import numpy as np
import ml_dtypes


def mxq(x, axis, fmt="e4m3"):
    dtype, down = {"e4m3": (ml_dtypes.float8_e4m3fn, 7), "e5m2": (ml_dtypes.float8_e5m2, 14)}[fmt]
    v = np.moveaxis(np.asarray(x, np.float32).astype(ml_dtypes.bfloat16).astype(np.float64), axis, -1)
    blocks = v.reshape(v.shape[:-1] + (-1, 32))
    amax = np.abs(blocks).max(-1, keepdims=True)
    byte = np.maximum(np.where(amax > 0, np.frexp(amax)[1] - 1 + 127, 0) - down, 1)
    scale = np.exp2(byte - 127.0)
    codes = (blocks / scale).astype(np.float32).astype(dtype).astype(np.float64)
    return np.moveaxis((codes * scale).reshape(v.shape), -1, axis)


WIDE = False


def mx_kscale(k):
    if not WIDE:
        return np.ones(k)
    levels = np.array([10, -10, 5, -5, 0])
    if k % 512:
        return np.exp2(np.random.permutation(np.resize(levels, k // 32))).repeat(32)
    a = np.empty((k // 512, 16))
    for p in range(k // 512):
        a[p, :8] = np.random.permutation(np.resize(levels, 8))
        for g in range(8):
            far = levels[np.abs(levels - a[p, g]) >= 10]
            a[p, g + 8] = far[np.random.randint(len(far))]
    return np.exp2(a.ravel()).repeat(32)


def f64(x):
    return np.asarray(x).astype(np.float64)


def striped(idx):
    return np.tile(idx.reshape(-1, 16).T, (8, 1)).astype(np.uint16)


def unstriped(offs):
    return offs[:16].T.reshape(-1).astype(np.int64)


def striped8(idx):
    return np.concatenate([x.reshape(-1, 16).T for x in idx]).astype(np.uint16)


def runs(offs, k):
    lists = np.stack([offs[16 * r : 16 * r + 16].T.reshape(-1) for r in range(8)]).astype(np.int64)
    return lists[np.arange(k) % 512 // 64]


def pack_weight(w):
    k, n = w.shape
    w = f64(np.asarray(w, np.float32).astype(ml_dtypes.bfloat16)).reshape(k // 32, 32, n)
    amax = np.abs(w).max(1)
    byte = np.clip(np.where(amax > 0, np.frexp(amax)[1] - 1 + 127 - 7, 1), 1, 254)
    scaled = (w * np.exp2(127.0 - byte)[:, None, :]).reshape(k, n).astype(np.float32)
    words = np.ascontiguousarray(scaled.reshape(k // 512, 128, 4, n).transpose(0, 1, 3, 2)).astype(ml_dtypes.float8_e4m3fn).view(np.uint8)
    return words, np.ascontiguousarray(byte.astype(np.uint8).reshape(k // 512, 16, n))


def unpack_weight(words, scales):
    g, p, n, _ = words.shape
    vals = np.ascontiguousarray(words).view(ml_dtypes.float8_e4m3fn).astype(np.float64) * np.repeat(np.exp2(scales.astype(np.float64) - 127.0), 8, axis=1)[..., None]
    return vals.transpose(0, 1, 3, 2).reshape(g * 512, n)


K, T, S, V, N, H = 512, 2048, 512, 256, 512, 512
P = 2 ** 7


def setup_inputs():
    n = np.random.standard_normal
    s = mx_kscale(K)[:, None]
    u = mx_kscale(S)
    packed_xT = pack_weight(n((K, T)) * s)
    perm = np.stack([np.random.permutation(H) for _ in range(8)])
    return {
        "x_words": packed_xT[0],
        "x_scales": packed_xT[1],
        "wa": (n((K, H)) / np.sqrt(K) / s).astype(np.float32),
        "cs": np.tile(np.random.uniform(0.3, 0.9, V), (P, 1)).astype(np.float32),
        "sn": np.tile(np.random.uniform(-0.9, -0.3, V), (P, 1)).astype(np.float32),
        "gt": (np.random.uniform(0.5, 1.5, (S, 1)) * u[:, None]).astype(np.float32),
        "w1": (n((S, N)) / np.sqrt(S) / u[:, None]).astype(np.float32),
        "offs": striped(np.random.permutation(T)[:S]),
        "la": striped8(perm[:, :V]),
        "lb": striped8(perm[:, V:]),
    }


def reference(x_words, x_scales, wa, cs, sn, gt, w1, offs, la, lb):
    xq = unpack_weight(x_words, x_scales)[:, unstriped(offs)]
    y = xq.T @ mxq(f64(wa), 0, "e4m3")
    a = y[np.arange(S)[:, None], runs(la, S)]
    b = y[np.arange(S)[:, None], runs(lb, S)]
    r2 = f64(sn)[:1] * a + f64(cs)[:1] * b
    r1 = f64(cs)[:1] * a - (f64(sn)[:1] * b)
    p = np.zeros((S, H))
    p[np.arange(S)[:, None], runs(la, S)] = r1
    d = p.copy()
    d[np.arange(S)[:, None], runs(lb, S)] = r2
    z = f64(gt) * d
    return mxq(f64(w1), 0, "e4m3").T @ mxq(z, 0, "e4m3")

@@ -1,0 +1,181 @@
+from contextlib import ExitStack
+
+import concourse.mybir as mybir
+from concourse.masks import make_identity
+
+K, T, S, V, N, H = 512, 2048, 512, 256, 512, 512
+FLOPS = 2 * K * S * H + 2 * S * N * H
+
+F32 = mybir.dt.float32
+BF16 = mybir.dt.bfloat16
+I32 = mybir.dt.int32
+U32 = mybir.dt.uint32
+U16 = mybir.dt.uint16
+U8 = mybir.dt.uint8
+FP8X4 = mybir.dt.float8_e4m3fn_x4
+COPY = mybir.ActivationFunctionType.Copy
+MULT = mybir.AluOpType.mult
+ADD = mybir.AluOpType.add
+
+P = 128
+PACK = 4
+HALF = 256
+V_SHARE = 160
+ORDER = (1, 3, 0, 2)
+
+
+def interleave(engine_copy, grouped, raw):
+    engine_copy(
+        out=grouped.rearrange("p (c i) t -> p c t i", i=4),
+        in_=raw.rearrange("p t (c i) -> p c t i", i=4),
+    )
+
+
+def tile_picked_featrot_none_p_kernel(tc, x_words, x_scales, wa, cs, sn, gt, w1, offs, la, lb, out):
+    nc = tc.nc
+    with ExitStack() as ctx:
+        keep = ctx.enter_context(tc.tile_pool(name="keep", bufs=1))
+        psum = ctx.enter_context(tc.psum_pool(name="psum", bufs=8))
+
+        offs_t = keep.tile([P, S // 16], U16, name="offs_t")
+        la_t = keep.tile([P, V // 16], U16, name="la_t")
+        lb_t = keep.tile([P, V // 16], U16, name="lb_t")
+        xw = keep.tile([P, T], I32, name="xw", align_bytes=64)
+        xs = keep.tile([P, T], U8, name="xs", align_bytes=64)
+        wa_raw = [keep.tile([P, PACK, HALF], F32, name="wa_raw%d" % h, align_bytes=64) for h in range(2)]
+        w1_raw = keep.tile([P, PACK, N], F32, name="w1_raw", align_bytes=64)
+        cs_col = keep.tile([P, 2], F32, name="cs_col")
+        sn_col = keep.tile([P, 2], F32, name="sn_col")
+        nsn_col = keep.tile([P, 2], F32, name="nsn_col")
+        gt_col = keep.tile([P, PACK], F32, name="gt_col")
+        ident = keep.tile([P, P], F32, name="ident", align_bytes=64)
+
+        nc.gpsimd.memset(xs[:].bitcast(I32), 0)
+        nc.sync.dma_start(offs_t[:], offs)
+        nc.sync.dma_start(la_t[:], la)
+        for q in range(4):
+            queue = nc.scalar if q < 2 else nc.sync
+            queue.dma_start(out=xs[32 * q : 32 * q + 4, :].bitcast(I32), in_=x_scales[0, 4 * q : 4 * q + 4, :].bitcast(I32))
+        nc.sync.dma_start(out=xw[:], in_=x_words[0].rearrange("p n t -> p (n t)").bitcast(I32))
+        wa_v = wa.rearrange("(p t) j -> p t j", t=PACK)
+        for h in range(2):
+            nc.sync.dma_start(out=wa_raw[h][:], in_=wa_v[:, :, h * HALF : (h + 1) * HALF])
+        nc.sync.dma_start(lb_t[:], lb)
+        with nc.allow_non_contiguous_dma(reason="one value a partition"):
+            nc.sync.dma_start(out=gt_col[:], in_=gt.rearrange("(p t) o -> p (t o)", t=PACK))
+            nc.sync.dma_start(out=sn_col[:], in_=sn[0].rearrange("(h p) -> p h", p=P))
+            nc.sync.dma_start(out=cs_col[:], in_=cs[0].rearrange("(h p) -> p h", p=P))
+        nc.sync.dma_start(out=w1_raw[:], in_=w1.rearrange("(p t) m -> p t m", t=PACK))
+        make_identity(nc, ident[:])
+        nc.gpsimd.tensor_scalar(out=nsn_col[:], in0=sn_col[:], scalar1=-1.0, scalar2=0.0, op0=MULT, op1=ADD)
+
+        def scalar_copy(out, in_):
+            nc.scalar.activation(out=out, in_=in_, func=COPY)
+
+        xs_picked = keep.tile([P, S], U8, name="xs_picked", align_bytes=64)
+        xs_dealt = keep.tile([P, PACK, P], U8, name="xs_dealt", align_bytes=64)
+        xw_dealt = keep.tile([P, PACK, P], U32, name="xw_dealt", align_bytes=64)
+        nc.vector.tensor_copy(xs_picked[:], xs[:].indirect(offs_t[:]))
+        nc.vector.tensor_copy(xw_dealt[:].rearrange("p t m -> p m t"), xw[:].bitcast(U32).indirect(offs_t[:]))
+        nc.vector.tensor_copy(out=xs_dealt[:].rearrange("p t m -> p m t"), in_=xs_picked[:].rearrange("p (m t) -> p m t", t=PACK))
+
+        y = [keep.tile([P, H], F32, name="y%d" % t, align_bytes=64) for t in range(PACK)]
+        y_bank = [psum.tile([P, H], F32, name="bank") for t in range(PACK)]
+        y_last = psum.tile([P, H], F32, name="bank")
+        first = ORDER[0]
+        wa_c = []
+        wa_s = []
+        for h in range(2):
+            grouped = keep.tile([P, HALF, PACK], BF16, name="wa_g%d" % h, align_bytes=64)
+            codes = keep.tile([P, HALF], U32, name="wa_c%d" % h, align_bytes=64)
+            scales = keep.tile([P, HALF], U8, name="wa_s%d" % h, align_bytes=64)
+            interleave(nc.vector.tensor_copy, grouped[:, :V_SHARE, :], wa_raw[h][:, :, :V_SHARE])
+            interleave(scalar_copy, grouped[:, V_SHARE:, :], wa_raw[h][:, :, V_SHARE:])
+            nc.vector.quantize_mx(out=codes[:].bitcast(FP8X4), scales=scales[:], in_=grouped[:].rearrange("p c t -> p (c t)"))
+            wa_c.append(codes)
+            wa_s.append(scales)
+        for t in ORDER:
+            for h in range(2):
+                cols = slice(h * HALF, (h + 1) * HALF)
+                bank = y_last if (h == 1 and t == first) else y_bank[t]
+                nc.tensor.matmul_mx(
+                    out=bank[:, cols], lhsT=xw_dealt[:, t, :].bitcast(FP8X4), lhsT_scale=xs_dealt[:, t, :],
+                    rhs=wa_c[h][:].bitcast(FP8X4), rhs_scale=wa_s[h][:], start=True, stop=True)
+        nc.scalar.activation(out=y[first][:, :HALF], in_=y_bank[first][:, :HALF], func=COPY, scale=gt_col[:, first : first + 1])
+        nc.vector.tensor_scalar(out=y[first][:, HALF:], in0=y_last[:, HALF:], scalar1=gt_col[:, first : first + 1], scalar2=None, op0=MULT)
+        for t in ORDER[1:]:
+            nc.scalar.activation(out=y[t][:], in_=y_bank[t][:], func=COPY, scale=gt_col[:, t : t + 1])
+
+        a = [keep.tile([P, V], F32, name="a%d" % t, align_bytes=64) for t in range(PACK)]
+        b = [keep.tile([P, V], F32, name="b%d" % t, align_bytes=64) for t in range(PACK)]
+        for t in ORDER:
+            nc.vector.tensor_copy(a[t][:], y[t][:].indirect(la_t[:]))
+            nc.vector.tensor_copy(b[t][:], y[t][:].indirect(lb_t[:]))
+
+        d = [keep.tile([P, H * (2 - t % 2)], F32, name="d%d" % t, align_bytes=64) for t in range(PACK)]
+
+        def rotate(t):
+            turned = psum.tile([P, 4, P], F32, name="bank")
+            for h in range(2):
+                nc.tensor.transpose(turned[:, 2 * h, :], a[t][:, h * P : (h + 1) * P], ident[:])
+                nc.tensor.transpose(turned[:, 2 * h + 1, :], b[t][:, h * P : (h + 1) * P], ident[:])
+            c_ab = keep.tile([P, 2, 2, P], F32, name="c_ab%d" % t, align_bytes=64)
+            ns_b = keep.tile([P, 2, P], F32, name="ns_b%d" % t, align_bytes=64)
+            s_a = keep.tile([P, 2, P], F32, name="s_a%d" % t, align_bytes=64)
+            for h in range(2):
+                nc.scalar.activation(out=c_ab[:, h, :, :], in_=turned[:, 2 * h : 2 * h + 2, :], func=COPY, scale=cs_col[:, h : h + 1])
+                nc.scalar.activation(out=ns_b[:, h, :], in_=turned[:, 2 * h + 1, :], func=COPY, scale=nsn_col[:, h : h + 1])
+            for h in range(2):
+                nc.scalar.activation(out=s_a[:, h, :], in_=turned[:, 2 * h, :], func=COPY, scale=sn_col[:, h : h + 1])
+            for which, other, lst in ((0, ns_b, la_t), (1, s_a, lb_t)):
+                acc = psum.tile([P, H], F32, name="bank")
+                for h in range(2):
+                    cols = acc[:, h * P : (h + 1) * P]
+                    nc.tensor.matmul(out=cols, lhsT=c_ab[:, h, which, :], rhs=ident[:], is_transpose=True, start=True, stop=False)
+                    nc.tensor.matmul(out=cols, lhsT=other[:, h, :], rhs=ident[:], is_transpose=True, start=False, stop=True)
+                r = keep.tile([P, V], F32, name="r%d%d" % (which, t), align_bytes=64)
+                nc.scalar.copy(out=r[:], in_=acc[:, :V])
+                nc.vector.tensor_copy(d[t][:].indirect(lst[:]), r[:])
+            if t % 2 == 1:
+                nc.sync.dma_start(out=d[t - 1][:, H:], in_=d[t][:])
+
+        for t in ORDER:
+            rotate(t)
+
+        w1_g = keep.tile([P, N, PACK], BF16, name="w1_g", tag="c_ab0", align_bytes=64)
+        w1_c = keep.tile([P, N], U32, name="w1_c", align_bytes=64)
+        w1_s = keep.tile([P, N], U8, name="w1_s", align_bytes=64)
+        for h in range(2):
+            interleave(nc.scalar.copy, w1_g[:, h * HALF : (h + 1) * HALF, :], w1_raw[:, :, h * HALF : (h + 1) * HALF])
+        nc.vector.quantize_mx(out=w1_c[:].bitcast(FP8X4), scales=w1_s[:], in_=w1_g[:].rearrange("p c t -> p (c t)"))
+
+        z_g = [keep.tile([P, HALF, PACK], BF16, name="z_g%d" % h, tag=("c_ab2", "s_a2")[h], align_bytes=64) for h in range(2)]
+
+        def pair(copy, t, h):
+            both = d[t][:].rearrange("p (e j) -> p e j", e=2)
+            cols = slice(h * HALF, (h + 1) * HALF)
+            copy(out=z_g[h][:, :, t : t + 2], in_=both[:, :, cols].rearrange("p e j -> p j e"))
+
+        for h in range(2):
+            pair(nc.scalar.copy, 0, h)
+        pair(nc.vector.tensor_copy, 2, 0)
+        pair(nc.scalar.copy, 2, 1)
+
+        out_v = out.rearrange("(u p) j -> p u j", p=P)
+        for h in range(2):
+            z_c = keep.tile([P, HALF], U32, name="z_c%d" % h, align_bytes=64)
+            z_s = keep.tile([P, HALF], U8, name="z_s%d" % h, align_bytes=64)
+            nc.vector.quantize_mx(out=z_c[:].bitcast(FP8X4), scales=z_s[:], in_=z_g[h][:].rearrange("p c t -> p (c t)"))
+            groups = ((0, 2), (2, 4)) if h == 0 else ((0, 2), (2, 3), (3, 4))
+            for g, (u0, u1) in enumerate(groups):
+                bank = psum.tile([P, 2, HALF], F32, name="bank")
+                for u in range(u0, u1):
+                    nc.tensor.matmul_mx(
+                        out=bank[:, u - u0, :], lhsT=w1_c[:, u * P : (u + 1) * P].bitcast(FP8X4), lhsT_scale=w1_s[:, u * P : (u + 1) * P],
+                        rhs=z_c[:].bitcast(FP8X4), rhs_scale=z_s[:], start=True, stop=True)
+                res = keep.tile([P, u1 - u0, HALF], F32, name="res%d%d" % (h, g), align_bytes=64)
+                if g == 1:
+                    nc.scalar.copy(out=res[:], in_=bank[:, : u1 - u0, :])
+                else:
+                    nc.vector.tensor_copy(out=res[:], in_=bank[:, : u1 - u0, :])
+                nc.sync.dma_start(out=out_v[:, u0:u1, h * HALF : (h + 1) * HALF], in_=res[:])

@@ -22,6 +22,7 @@ PACK = 4
 HALF = 256
 V_SHARE = 160
 ORDER = (1, 3, 0, 2)
+QUARTER = 128
 
 
 def interleave(engine_copy, grouped, raw):
@@ -114,68 +115,91 @@ def tile_picked_featrot_none_p_kernel(tc, x_words, x_scales, wa, cs, sn, gt, w1,
 
         d = [keep.tile([P, H * (2 - t % 2)], F32, name="d%d" % t, align_bytes=64) for t in range(PACK)]
 
-        def rotate(t):
-            turned = psum.tile([P, 4, P], F32, name="bank")
+        def rotate(t, between=None):
+            c_ab = []
+            ns_b = []
+            turned = []
             for h in range(2):
-                nc.tensor.transpose(turned[:, 2 * h, :], a[t][:, h * P : (h + 1) * P], ident[:])
-                nc.tensor.transpose(turned[:, 2 * h + 1, :], b[t][:, h * P : (h + 1) * P], ident[:])
-            c_ab = keep.tile([P, 2, 2, P], F32, name="c_ab%d" % t, align_bytes=64)
-            ns_b = keep.tile([P, 2, P], F32, name="ns_b%d" % t, align_bytes=64)
-            s_a = keep.tile([P, 2, P], F32, name="s_a%d" % t, align_bytes=64)
+                bank = psum.tile([P, 2, P], F32, name="bank")
+                nc.tensor.transpose(bank[:, 0, :], a[t][:, h * P : (h + 1) * P], ident[:])
+                nc.tensor.transpose(bank[:, 1, :], b[t][:, h * P : (h + 1) * P], ident[:])
+                turned.append(bank)
             for h in range(2):
-                nc.scalar.activation(out=c_ab[:, h, :, :], in_=turned[:, 2 * h : 2 * h + 2, :], func=COPY, scale=cs_col[:, h : h + 1])
-                nc.scalar.activation(out=ns_b[:, h, :], in_=turned[:, 2 * h + 1, :], func=COPY, scale=nsn_col[:, h : h + 1])
-            for h in range(2):
-                nc.scalar.activation(out=s_a[:, h, :], in_=turned[:, 2 * h, :], func=COPY, scale=sn_col[:, h : h + 1])
-            for which, other, lst in ((0, ns_b, la_t), (1, s_a, lb_t)):
-                acc = psum.tile([P, H], F32, name="bank")
+                c_ab.append(keep.tile([P, 2, P], F32, name="c_ab%d%d" % (t, h), align_bytes=64))
+                ns_b.append(keep.tile([P, P], F32, name="sin%d%d" % (t, h), align_bytes=64))
+                nc.scalar.activation(out=c_ab[h][:], in_=turned[h][:], func=COPY, scale=cs_col[:, h : h + 1])
+                nc.scalar.activation(out=ns_b[h][:], in_=turned[h][:, 1, :], func=COPY, scale=nsn_col[:, h : h + 1])
+
+            def back(which, other):
+                acc = psum.tile([P, V], F32, name="bank")
                 for h in range(2):
                     cols = acc[:, h * P : (h + 1) * P]
-                    nc.tensor.matmul(out=cols, lhsT=c_ab[:, h, which, :], rhs=ident[:], is_transpose=True, start=True, stop=False)
-                    nc.tensor.matmul(out=cols, lhsT=other[:, h, :], rhs=ident[:], is_transpose=True, start=False, stop=True)
+                    nc.tensor.matmul(out=cols, lhsT=c_ab[h][:, which, :], rhs=ident[:], is_transpose=True, start=True, stop=False)
+                    nc.tensor.matmul(out=cols, lhsT=other[h][:], rhs=ident[:], is_transpose=True, start=False, stop=True)
                 r = keep.tile([P, V], F32, name="r%d%d" % (which, t), align_bytes=64)
-                nc.scalar.copy(out=r[:], in_=acc[:, :V])
-                nc.vector.tensor_copy(d[t][:].indirect(lst[:]), r[:])
+                nc.scalar.copy(out=r[:], in_=acc[:])
+                return r
+
+            r1 = back(0, ns_b)
+            nc.vector.tensor_copy(d[t][:].indirect(la_t[:]), r1[:])
+            s_a = []
+            for h in range(2):
+                s_a.append(keep.tile([P, P], F32, name="sin%d%d" % (t, h), align_bytes=64))
+                nc.scalar.activation(out=s_a[h][:], in_=turned[h][:, 0, :], func=COPY, scale=sn_col[:, h : h + 1])
+            r2 = back(1, s_a)
+            if between is not None:
+                between()
+            nc.vector.tensor_copy(d[t][:].indirect(lb_t[:]), r2[:])
             if t % 2 == 1:
                 nc.sync.dma_start(out=d[t - 1][:, H:], in_=d[t][:])
+            return r1
 
-        for t in ORDER:
-            rotate(t)
+        w1_c = []
+        w1_s = []
 
-        w1_g = keep.tile([P, N, PACK], BF16, name="w1_g", tag="c_ab0", align_bytes=64)
-        w1_c = keep.tile([P, N], U32, name="w1_c", align_bytes=64)
-        w1_s = keep.tile([P, N], U8, name="w1_s", align_bytes=64)
-        for h in range(2):
-            interleave(nc.scalar.copy, w1_g[:, h * HALF : (h + 1) * HALF, :], w1_raw[:, :, h * HALF : (h + 1) * HALF])
-        nc.vector.quantize_mx(out=w1_c[:].bitcast(FP8X4), scales=w1_s[:], in_=w1_g[:].rearrange("p c t -> p (c t)"))
+        def w1_half(h, after, inside):
+            grouped = keep.tile([P, HALF, PACK], BF16, name="w1_g%d" % h, tag="c_ab%d1" % after, align_bytes=64)
+            interleave(nc.scalar.copy, grouped[:], w1_raw[:, :, h * HALF : (h + 1) * HALF])
 
-        z_g = [keep.tile([P, HALF, PACK], BF16, name="z_g%d" % h, tag=("c_ab2", "s_a2")[h], align_bytes=64) for h in range(2)]
+            def quantise():
+                codes = keep.tile([P, HALF], U32, name="w1_c%d" % h, tag="sin%d1" % inside, align_bytes=64)
+                scales = keep.tile([P, HALF], U8, name="w1_s%d" % h, align_bytes=64)
+                nc.vector.quantize_mx(out=codes[:].bitcast(FP8X4), scales=scales[:], in_=grouped[:].rearrange("p c t -> p (c t)"))
+                w1_c.append(codes)
+                w1_s.append(scales)
 
-        def pair(copy, t, h):
+            return quantise
+
+        rotate(ORDER[0])
+        rotate(ORDER[1])
+        rotate(ORDER[2], w1_half(0, ORDER[1], ORDER[2]))
+        rotate(ORDER[3], w1_half(1, ORDER[2], ORDER[3]))
+        last = ORDER[3]
+        z_g = keep.tile([P, H, PACK], BF16, name="z_g", tag="c_ab%d1" % last, align_bytes=64)
+
+        def pair(copy, t, c0, c1):
             both = d[t][:].rearrange("p (e j) -> p e j", e=2)
-            cols = slice(h * HALF, (h + 1) * HALF)
-            copy(out=z_g[h][:, :, t : t + 2], in_=both[:, :, cols].rearrange("p e j -> p j e"))
+            copy(out=z_g[:, c0:c1, t : t + 2], in_=both[:, :, c0:c1].rearrange("p e j -> p j e"))
 
-        for h in range(2):
-            pair(nc.scalar.copy, 0, h)
-        pair(nc.vector.tensor_copy, 2, 0)
-        pair(nc.scalar.copy, 2, 1)
+        pair(nc.scalar.copy, 0, 0, H)
+        pair(nc.vector.tensor_copy, 2, 0, QUARTER)
+        pair(nc.vector.tensor_copy, 2, QUARTER, HALF)
+        pair(nc.scalar.copy, 2, HALF, H)
 
-        out_v = out.rearrange("(u p) j -> p u j", p=P)
+        z_c = [keep.tile([P, HALF], U32, name="z_c%d" % h, align_bytes=64) for h in range(2)]
+        z_s = [keep.tile([P, HALF], U8, name="z_s%d" % h, align_bytes=64) for h in range(2)]
+        for c0, c1 in ((0, QUARTER), (QUARTER, HALF), (HALF, H)):
+            h = c0 // HALF
+            cols = slice(c0 - h * HALF, c1 - h * HALF)
+            nc.vector.quantize_mx(out=z_c[h][:, cols].bitcast(FP8X4), scales=z_s[h][:, cols], in_=z_g[:, c0:c1, :].rearrange("p c t -> p (c t)"))
         for h in range(2):
-            z_c = keep.tile([P, HALF], U32, name="z_c%d" % h, align_bytes=64)
-            z_s = keep.tile([P, HALF], U8, name="z_s%d" % h, align_bytes=64)
-            nc.vector.quantize_mx(out=z_c[:].bitcast(FP8X4), scales=z_s[:], in_=z_g[h][:].rearrange("p c t -> p (c t)"))
-            groups = ((0, 2), (2, 4)) if h == 0 else ((0, 2), (2, 3), (3, 4))
-            for g, (u0, u1) in enumerate(groups):
-                bank = psum.tile([P, 2, HALF], F32, name="bank")
-                for u in range(u0, u1):
-                    nc.tensor.matmul_mx(
-                        out=bank[:, u - u0, :], lhsT=w1_c[:, u * P : (u + 1) * P].bitcast(FP8X4), lhsT_scale=w1_s[:, u * P : (u + 1) * P],
-                        rhs=z_c[:].bitcast(FP8X4), rhs_scale=z_s[:], start=True, stop=True)
-                res = keep.tile([P, u1 - u0, HALF], F32, name="res%d%d" % (h, g), align_bytes=64)
-                if g == 1:
-                    nc.scalar.copy(out=res[:], in_=bank[:, : u1 - u0, :])
-                else:
-                    nc.vector.tensor_copy(out=res[:], in_=bank[:, : u1 - u0, :])
-                nc.sync.dma_start(out=out_v[:, u0:u1, h * HALF : (h + 1) * HALF], in_=res[:])
+            for u in range(PACK):
+                cols = slice((u % 2) * P, (u % 2 + 1) * P)
+                bank = psum.tile([P, HALF], F32, name="bank")
+                nc.tensor.matmul_mx(
+                    out=bank[:], lhsT=w1_c[u // 2][:, cols].bitcast(FP8X4), lhsT_scale=w1_s[u // 2][:, cols],
+                    rhs=z_c[h][:].bitcast(FP8X4), rhs_scale=z_s[h][:], start=True, stop=True)
+                res = keep.tile([P, HALF], F32, name="res%d%d" % (h, u), align_bytes=64)
+                copy = nc.vector.tensor_copy if u % 2 == 0 else nc.scalar.copy
+                copy(out=res[:], in_=bank[:])
+                nc.sync.dma_start(out=out[u * P : (u + 1) * P, h * HALF : (h + 1) * HALF], in_=res[:])

@@ -20,7 +20,7 @@ ADD = mybir.AluOpType.add
 P = 128
 PACK = 4
 HALF = 256
-V_SHARE = 160
+V_SHARE = (96, 160)
 ORDER = (1, 3, 0, 2)
 QUARTER = 128
 
@@ -82,6 +82,7 @@ def tile_picked_featrot_none_p_kernel(tc, x_words, x_scales, wa, cs, sn, gt, w1,
 
         y = [keep.tile([P, H], F32, name="y%d" % t, align_bytes=64) for t in range(PACK)]
         y_bank = [psum.tile([P, H], F32, name="bank") for t in range(PACK)]
+        y_third = psum.tile([P, H], F32, name="bank")
         y_last = psum.tile([P, H], F32, name="bank")
         first = ORDER[0]
         wa_c = []
@@ -90,20 +91,30 @@ def tile_picked_featrot_none_p_kernel(tc, x_words, x_scales, wa, cs, sn, gt, w1,
             grouped = keep.tile([P, HALF, PACK], BF16, name="wa_g%d" % h, align_bytes=64)
             codes = keep.tile([P, HALF], U32, name="wa_c%d" % h, align_bytes=64)
             scales = keep.tile([P, HALF], U8, name="wa_s%d" % h, align_bytes=64)
-            interleave(nc.vector.tensor_copy, grouped[:, :V_SHARE, :], wa_raw[h][:, :, :V_SHARE])
-            interleave(scalar_copy, grouped[:, V_SHARE:, :], wa_raw[h][:, :, V_SHARE:])
+            share = V_SHARE[h]
+            interleave(nc.vector.tensor_copy, grouped[:, :share, :], wa_raw[h][:, :, :share])
+            interleave(scalar_copy, grouped[:, share:, :], wa_raw[h][:, :, share:])
             nc.vector.quantize_mx(out=codes[:].bitcast(FP8X4), scales=scales[:], in_=grouped[:].rearrange("p c t -> p (c t)"))
             wa_c.append(codes)
             wa_s.append(scales)
-        for t in ORDER:
-            for h in range(2):
-                cols = slice(h * HALF, (h + 1) * HALF)
-                bank = y_last if (h == 1 and t == first) else y_bank[t]
-                nc.tensor.matmul_mx(
-                    out=bank[:, cols], lhsT=xw_dealt[:, t, :].bitcast(FP8X4), lhsT_scale=xs_dealt[:, t, :],
-                    rhs=wa_c[h][:].bitcast(FP8X4), rhs_scale=wa_s[h][:], start=True, stop=True)
-        nc.scalar.activation(out=y[first][:, :HALF], in_=y_bank[first][:, :HALF], func=COPY, scale=gt_col[:, first : first + 1])
-        nc.vector.tensor_scalar(out=y[first][:, HALF:], in0=y_last[:, HALF:], scalar1=gt_col[:, first : first + 1], scalar2=None, op0=MULT)
+        def project(bank, t, c0, c1):
+            h = c0 // HALF
+            cols = slice(c0 - h * HALF, c1 - h * HALF)
+            nc.tensor.matmul_mx(
+                out=bank[:, c0:c1], lhsT=xw_dealt[:, t, :].bitcast(FP8X4), lhsT_scale=xs_dealt[:, t, :],
+                rhs=wa_c[h][:, cols].bitcast(FP8X4), rhs_scale=wa_s[h][:, cols], start=True, stop=True)
+
+        third = HALF + QUARTER
+        project(y_bank[first], first, 0, HALF)
+        project(y_third, first, HALF, third)
+        project(y_last, first, third, H)
+        for t in ORDER[1:]:
+            project(y_bank[t], t, 0, HALF)
+            project(y_bank[t], t, HALF, H)
+        gt_first = gt_col[:, first : first + 1]
+        nc.scalar.activation(out=y[first][:, :HALF], in_=y_bank[first][:, :HALF], func=COPY, scale=gt_first)
+        nc.vector.tensor_scalar(out=y[first][:, HALF:third], in0=y_third[:, HALF:third], scalar1=gt_first, scalar2=None, op0=MULT)
+        nc.scalar.activation(out=y[first][:, third:], in_=y_last[:, third:], func=COPY, scale=gt_first)
         for t in ORDER[1:]:
             nc.scalar.activation(out=y[t][:], in_=y_bank[t][:], func=COPY, scale=gt_col[:, t : t + 1])
 
@@ -192,14 +203,19 @@ def tile_picked_featrot_none_p_kernel(tc, x_words, x_scales, wa, cs, sn, gt, w1,
             h = c0 // HALF
             cols = slice(c0 - h * HALF, c1 - h * HALF)
             nc.vector.quantize_mx(out=z_c[h][:, cols].bitcast(FP8X4), scales=z_s[h][:, cols], in_=z_g[:, c0:c1, :].rearrange("p c t -> p (c t)"))
-        for h in range(2):
-            for u in range(PACK):
+        out_v = out.rearrange("(u p) j -> p u j", p=P)
+        units = [(c0, c0 + QUARTER, u0, u0 + 2) for c0 in (0, QUARTER) for u0 in (0, 2)]
+        units = units + [(HALF, H, u, u + 1) for u in range(PACK)]
+        for i, (c0, c1, u0, u1) in enumerate(units):
+            h = c0 // HALF
+            z_cols = slice(c0 - h * HALF, c1 - h * HALF)
+            bank = psum.tile([P, u1 - u0, c1 - c0], F32, name="bank")
+            for u in range(u0, u1):
                 cols = slice((u % 2) * P, (u % 2 + 1) * P)
-                bank = psum.tile([P, HALF], F32, name="bank")
                 nc.tensor.matmul_mx(
-                    out=bank[:], lhsT=w1_c[u // 2][:, cols].bitcast(FP8X4), lhsT_scale=w1_s[u // 2][:, cols],
-                    rhs=z_c[h][:].bitcast(FP8X4), rhs_scale=z_s[h][:], start=True, stop=True)
-                res = keep.tile([P, HALF], F32, name="res%d%d" % (h, u), align_bytes=64)
-                copy = nc.vector.tensor_copy if u % 2 == 0 else nc.scalar.copy
-                copy(out=res[:], in_=bank[:])
-                nc.sync.dma_start(out=out[u * P : (u + 1) * P, h * HALF : (h + 1) * HALF], in_=res[:])
+                    out=bank[:, u - u0, :], lhsT=w1_c[u // 2][:, cols].bitcast(FP8X4), lhsT_scale=w1_s[u // 2][:, cols],
+                    rhs=z_c[h][:, z_cols].bitcast(FP8X4), rhs_scale=z_s[h][:, z_cols], start=True, stop=True)
+            res = keep.tile([P, u1 - u0, c1 - c0], F32, name="res%d" % i, align_bytes=64)
+            copy = nc.scalar.copy if i % 2 == 0 else nc.vector.tensor_copy
+            copy(out=res[:], in_=bank[:])
+            nc.sync.dma_start(out=out_v[:, u0:u1, c0:c1], in_=res[:])

@@ -118,11 +118,17 @@ def tile_picked_featrot_none_p_kernel(tc, x_words, x_scales, wa, cs, sn, gt, w1,
         for t in ORDER[1:]:
             nc.scalar.activation(out=y[t][:], in_=y_bank[t][:], func=COPY, scale=gt_col[:, t : t + 1])
 
-        a = [keep.tile([P, V], F32, name="a%d" % t, align_bytes=64) for t in range(PACK)]
-        b = [keep.tile([P, V], F32, name="b%d" % t, align_bytes=64) for t in range(PACK)]
-        for t in ORDER:
-            nc.vector.tensor_copy(a[t][:], y[t][:].indirect(la_t[:]))
-            nc.vector.tensor_copy(b[t][:], y[t][:].indirect(lb_t[:]))
+        a = {}
+        b = {}
+
+        def fetch(into, t, lst, tag):
+            into[t] = keep.tile([P, V], F32, name="picked", tag=tag, align_bytes=64)
+            nc.vector.tensor_copy(into[t][:], y[t][:].indirect(lst[:]))
+
+        for t in ORDER[:3]:
+            fetch(a, t, la_t, "a%d" % t)
+            fetch(b, t, lb_t, "b%d" % t)
+        fetch(a, ORDER[3], la_t, "a%d" % ORDER[3])
 
         d = [keep.tile([P, H * (2 - t % 2)], F32, name="d%d" % t, align_bytes=64) for t in range(PACK)]
 
@@ -181,7 +187,7 @@ def tile_picked_featrot_none_p_kernel(tc, x_words, x_scales, wa, cs, sn, gt, w1,
 
             return quantise
 
-        rotate(ORDER[0])
+        rotate(ORDER[0], lambda: fetch(b, ORDER[3], lb_t, "sin%d1" % ORDER[0]))
         rotate(ORDER[1])
         rotate(ORDER[2], w1_half(0, ORDER[1], ORDER[2]))
         rotate(ORDER[3], w1_half(1, ORDER[2], ORDER[3]))

from contextlib import ExitStack

import concourse.mybir as mybir
from concourse.masks import make_identity

K, T, S, V, N, H = 512, 2048, 512, 256, 512, 512
FLOPS = 2 * K * S * H + 2 * S * N * H

F32 = mybir.dt.float32
BF16 = mybir.dt.bfloat16
I32 = mybir.dt.int32
U32 = mybir.dt.uint32
U16 = mybir.dt.uint16
U8 = mybir.dt.uint8
FP8X4 = mybir.dt.float8_e4m3fn_x4
COPY = mybir.ActivationFunctionType.Copy
MULT = mybir.AluOpType.mult
ADD = mybir.AluOpType.add

P = 128
PACK = 4
HALF = 256
V_SHARE = (96, 160)
ORDER = (1, 3, 0, 2)
QUARTER = 128


def interleave(engine_copy, grouped, raw):
    engine_copy(
        out=grouped.rearrange("p (c i) t -> p c t i", i=4),
        in_=raw.rearrange("p t (c i) -> p c t i", i=4),
    )


def tile_picked_featrot_none_p_kernel(tc, x_words, x_scales, wa, cs, sn, gt, w1, offs, la, lb, out):
    nc = tc.nc
    with ExitStack() as ctx:
        keep = ctx.enter_context(tc.tile_pool(name="keep", bufs=1))
        psum = ctx.enter_context(tc.psum_pool(name="psum", bufs=8))

        offs_t = keep.tile([P, S // 16], U16, name="offs_t")
        la_t = keep.tile([P, V // 16], U16, name="la_t")
        lb_t = keep.tile([P, V // 16], U16, name="lb_t")
        xw = keep.tile([P, T], I32, name="xw", align_bytes=64)
        xs = keep.tile([P, T], U8, name="xs", align_bytes=64)
        wa_raw = [keep.tile([P, PACK, HALF], F32, name="wa_raw%d" % h, align_bytes=64) for h in range(2)]
        w1_raw = keep.tile([P, PACK, N], F32, name="w1_raw", align_bytes=64)
        cs_col = keep.tile([P, 2], F32, name="cs_col")
        sn_col = keep.tile([P, 2], F32, name="sn_col")
        nsn_col = keep.tile([P, 2], F32, name="nsn_col")
        gt_col = keep.tile([P, PACK], F32, name="gt_col")
        ident = keep.tile([P, P], F32, name="ident", align_bytes=64)

        nc.gpsimd.memset(xs[:].bitcast(I32), 0)
        nc.sync.dma_start(offs_t[:], offs)
        nc.sync.dma_start(la_t[:], la)
        for q in range(4):
            queue = nc.scalar if q < 2 else nc.sync
            queue.dma_start(out=xs[32 * q : 32 * q + 4, :].bitcast(I32), in_=x_scales[0, 4 * q : 4 * q + 4, :].bitcast(I32))
        nc.sync.dma_start(out=xw[:], in_=x_words[0].rearrange("p n t -> p (n t)").bitcast(I32))
        wa_v = wa.rearrange("(p t) j -> p t j", t=PACK)
        for h in range(2):
            nc.sync.dma_start(out=wa_raw[h][:], in_=wa_v[:, :, h * HALF : (h + 1) * HALF])
        nc.sync.dma_start(lb_t[:], lb)
        with nc.allow_non_contiguous_dma(reason="one value a partition"):
            nc.sync.dma_start(out=gt_col[:], in_=gt.rearrange("(p t) o -> p (t o)", t=PACK))
            nc.sync.dma_start(out=sn_col[:], in_=sn[0].rearrange("(h p) -> p h", p=P))
            nc.sync.dma_start(out=cs_col[:], in_=cs[0].rearrange("(h p) -> p h", p=P))
        nc.sync.dma_start(out=w1_raw[:], in_=w1.rearrange("(p t) m -> p t m", t=PACK))
        make_identity(nc, ident[:])
        nc.gpsimd.tensor_scalar(out=nsn_col[:], in0=sn_col[:], scalar1=-1.0, scalar2=0.0, op0=MULT, op1=ADD)

        def scalar_copy(out, in_):
            nc.scalar.activation(out=out, in_=in_, func=COPY)

        xs_picked = keep.tile([P, S], U8, name="xs_picked", align_bytes=64)
        xs_dealt = keep.tile([P, PACK, P], U8, name="xs_dealt", align_bytes=64)
        xw_dealt = keep.tile([P, PACK, P], U32, name="xw_dealt", align_bytes=64)
        nc.vector.tensor_copy(xs_picked[:], xs[:].indirect(offs_t[:]))
        nc.vector.tensor_copy(xw_dealt[:].rearrange("p t m -> p m t"), xw[:].bitcast(U32).indirect(offs_t[:]))
        nc.vector.tensor_copy(out=xs_dealt[:].rearrange("p t m -> p m t"), in_=xs_picked[:].rearrange("p (m t) -> p m t", t=PACK))

        y = [keep.tile([P, H], F32, name="y%d" % t, align_bytes=64) for t in range(PACK)]
        y_bank = [psum.tile([P, H], F32, name="bank") for t in range(PACK)]
        y_third = psum.tile([P, H], F32, name="bank")
        y_last = psum.tile([P, H], F32, name="bank")
        first = ORDER[0]
        wa_c = []
        wa_s = []
        for h in range(2):
            grouped = keep.tile([P, HALF, PACK], BF16, name="wa_g%d" % h, align_bytes=64)
            codes = keep.tile([P, HALF], U32, name="wa_c%d" % h, align_bytes=64)
            scales = keep.tile([P, HALF], U8, name="wa_s%d" % h, align_bytes=64)
            share = V_SHARE[h]
            interleave(nc.vector.tensor_copy, grouped[:, :share, :], wa_raw[h][:, :, :share])
            interleave(scalar_copy, grouped[:, share:, :], wa_raw[h][:, :, share:])
            nc.vector.quantize_mx(out=codes[:].bitcast(FP8X4), scales=scales[:], in_=grouped[:].rearrange("p c t -> p (c t)"))
            wa_c.append(codes)
            wa_s.append(scales)
        def project(bank, t, c0, c1):
            h = c0 // HALF
            cols = slice(c0 - h * HALF, c1 - h * HALF)
            nc.tensor.matmul_mx(
                out=bank[:, c0:c1], lhsT=xw_dealt[:, t, :].bitcast(FP8X4), lhsT_scale=xs_dealt[:, t, :],
                rhs=wa_c[h][:, cols].bitcast(FP8X4), rhs_scale=wa_s[h][:, cols], start=True, stop=True)

        third = HALF + QUARTER
        project(y_bank[first], first, 0, HALF)
        project(y_third, first, HALF, third)
        project(y_last, first, third, H)
        for t in ORDER[1:]:
            project(y_bank[t], t, 0, HALF)
            project(y_bank[t], t, HALF, H)
        gt_first = gt_col[:, first : first + 1]
        nc.scalar.activation(out=y[first][:, :HALF], in_=y_bank[first][:, :HALF], func=COPY, scale=gt_first)
        nc.vector.tensor_scalar(out=y[first][:, HALF:third], in0=y_third[:, HALF:third], scalar1=gt_first, scalar2=None, op0=MULT)
        nc.scalar.activation(out=y[first][:, third:], in_=y_last[:, third:], func=COPY, scale=gt_first)
        for t in ORDER[1:]:
            nc.scalar.activation(out=y[t][:], in_=y_bank[t][:], func=COPY, scale=gt_col[:, t : t + 1])

        a = {}
        b = {}

        def fetch(into, t, lst, tag):
            into[t] = keep.tile([P, V], F32, name="picked", tag=tag, align_bytes=64)
            nc.vector.tensor_copy(into[t][:], y[t][:].indirect(lst[:]))

        for t in ORDER[:3]:
            fetch(a, t, la_t, "a%d" % t)
            fetch(b, t, lb_t, "b%d" % t)
        fetch(a, ORDER[3], la_t, "a%d" % ORDER[3])

        d = [keep.tile([P, H * (2 - t % 2)], F32, name="d%d" % t, align_bytes=64) for t in range(PACK)]

        def rotate(t, between=None):
            c_ab = []
            ns_b = []
            turned = []
            for h in range(2):
                bank = psum.tile([P, 2, P], F32, name="bank")
                nc.tensor.transpose(bank[:, 0, :], a[t][:, h * P : (h + 1) * P], ident[:])
                nc.tensor.transpose(bank[:, 1, :], b[t][:, h * P : (h + 1) * P], ident[:])
                turned.append(bank)
            for h in range(2):
                c_ab.append(keep.tile([P, 2, P], F32, name="c_ab%d%d" % (t, h), align_bytes=64))
                ns_b.append(keep.tile([P, P], F32, name="sin%d%d" % (t, h), align_bytes=64))
                nc.scalar.activation(out=c_ab[h][:], in_=turned[h][:], func=COPY, scale=cs_col[:, h : h + 1])
                nc.scalar.activation(out=ns_b[h][:], in_=turned[h][:, 1, :], func=COPY, scale=nsn_col[:, h : h + 1])

            def back(which, other):
                acc = psum.tile([P, V], F32, name="bank")
                for h in range(2):
                    cols = acc[:, h * P : (h + 1) * P]
                    nc.tensor.matmul(out=cols, lhsT=c_ab[h][:, which, :], rhs=ident[:], is_transpose=True, start=True, stop=False)
                    nc.tensor.matmul(out=cols, lhsT=other[h][:], rhs=ident[:], is_transpose=True, start=False, stop=True)
                r = keep.tile([P, V], F32, name="r%d%d" % (which, t), align_bytes=64)
                nc.scalar.copy(out=r[:], in_=acc[:])
                return r

            r1 = back(0, ns_b)
            nc.vector.tensor_copy(d[t][:].indirect(la_t[:]), r1[:])
            s_a = []
            for h in range(2):
                s_a.append(keep.tile([P, P], F32, name="sin%d%d" % (t, h), align_bytes=64))
                nc.scalar.activation(out=s_a[h][:], in_=turned[h][:, 0, :], func=COPY, scale=sn_col[:, h : h + 1])
            r2 = back(1, s_a)
            if between is not None:
                between()
            nc.vector.tensor_copy(d[t][:].indirect(lb_t[:]), r2[:])
            if t % 2 == 1:
                nc.sync.dma_start(out=d[t - 1][:, H:], in_=d[t][:])
            return r1

        w1_c = []
        w1_s = []

        def w1_half(h, after, inside):
            grouped = keep.tile([P, HALF, PACK], BF16, name="w1_g%d" % h, tag="c_ab%d1" % after, align_bytes=64)
            interleave(nc.scalar.copy, grouped[:], w1_raw[:, :, h * HALF : (h + 1) * HALF])

            def quantise():
                codes = keep.tile([P, HALF], U32, name="w1_c%d" % h, tag="sin%d1" % inside, align_bytes=64)
                scales = keep.tile([P, HALF], U8, name="w1_s%d" % h, align_bytes=64)
                nc.vector.quantize_mx(out=codes[:].bitcast(FP8X4), scales=scales[:], in_=grouped[:].rearrange("p c t -> p (c t)"))
                w1_c.append(codes)
                w1_s.append(scales)

            return quantise

        rotate(ORDER[0], lambda: fetch(b, ORDER[3], lb_t, "sin%d1" % ORDER[0]))
        rotate(ORDER[1])
        rotate(ORDER[2], w1_half(0, ORDER[1], ORDER[2]))
        rotate(ORDER[3], w1_half(1, ORDER[2], ORDER[3]))
        last = ORDER[3]
        z_g = keep.tile([P, H, PACK], BF16, name="z_g", tag="c_ab%d1" % last, align_bytes=64)

        def pair(copy, t, c0, c1):
            both = d[t][:].rearrange("p (e j) -> p e j", e=2)
            copy(out=z_g[:, c0:c1, t : t + 2], in_=both[:, :, c0:c1].rearrange("p e j -> p j e"))

        pair(nc.scalar.copy, 0, 0, H)
        pair(nc.vector.tensor_copy, 2, 0, QUARTER)
        pair(nc.vector.tensor_copy, 2, QUARTER, HALF)
        pair(nc.scalar.copy, 2, HALF, H)

        z_c = [keep.tile([P, HALF], U32, name="z_c%d" % h, align_bytes=64) for h in range(2)]
        z_s = [keep.tile([P, HALF], U8, name="z_s%d" % h, align_bytes=64) for h in range(2)]
        for c0, c1 in ((0, QUARTER), (QUARTER, HALF), (HALF, H)):
            h = c0 // HALF
            cols = slice(c0 - h * HALF, c1 - h * HALF)
            nc.vector.quantize_mx(out=z_c[h][:, cols].bitcast(FP8X4), scales=z_s[h][:, cols], in_=z_g[:, c0:c1, :].rearrange("p c t -> p (c t)"))
        out_v = out.rearrange("(u p) j -> p u j", p=P)
        units = [(c0, c0 + QUARTER, u0, u0 + 2) for c0 in (0, QUARTER) for u0 in (0, 2)]
        units = units + [(HALF, H, u, u + 1) for u in range(PACK)]
        for i, (c0, c1, u0, u1) in enumerate(units):
            h = c0 // HALF
            z_cols = slice(c0 - h * HALF, c1 - h * HALF)
            bank = psum.tile([P, u1 - u0, c1 - c0], F32, name="bank")
            for u in range(u0, u1):
                cols = slice((u % 2) * P, (u % 2 + 1) * P)
                nc.tensor.matmul_mx(
                    out=bank[:, u - u0, :], lhsT=w1_c[u // 2][:, cols].bitcast(FP8X4), lhsT_scale=w1_s[u // 2][:, cols],
                    rhs=z_c[h][:, z_cols].bitcast(FP8X4), rhs_scale=z_s[h][:, z_cols], start=True, stop=True)
            res = keep.tile([P, u1 - u0, c1 - c0], F32, name="res%d" % i, align_bytes=64)
            copy = nc.scalar.copy if i % 2 == 0 else nc.vector.tensor_copy
            copy(out=res[:], in_=bank[:])
            nc.sync.dma_start(out=out_v[:, u0:u1, c0:c1], in_=res[:])
